import numpy as np
import ml_dtypes


def mxq(x, axis, fmt="e4m3"):
    dtype, down = {"e4m3": (ml_dtypes.float8_e4m3fn, 7), "e5m2": (ml_dtypes.float8_e5m2, 14)}[fmt]
    v = np.moveaxis(np.asarray(x, np.float32).astype(ml_dtypes.bfloat16).astype(np.float64), axis, -1)
    blocks = v.reshape(v.shape[:-1] + (-1, 32))
    amax = np.abs(blocks).max(-1, keepdims=True)
    byte = np.maximum(np.where(amax > 0, np.frexp(amax)[1] - 1 + 127, 0) - down, 1)
    scale = np.exp2(byte - 127.0)
    codes = (blocks / scale).astype(np.float32).astype(dtype).astype(np.float64)
    return np.moveaxis((codes * scale).reshape(v.shape), -1, axis)


WIDE = False


def mx_kscale(k):
    if not WIDE:
        return np.ones(k)
    levels = np.array([10, -10, 5, -5, 0])
    if k % 512:
        return np.exp2(np.random.permutation(np.resize(levels, k // 32))).repeat(32)
    a = np.empty((k // 512, 16))
    for p in range(k // 512):
        a[p, :8] = np.random.permutation(np.resize(levels, 8))
        for g in range(8):
            far = levels[np.abs(levels - a[p, g]) >= 10]
            a[p, g + 8] = far[np.random.randint(len(far))]
    return np.exp2(a.ravel()).repeat(32)


def f64(x):
    return np.asarray(x).astype(np.float64)


def striped(idx):
    return np.tile(idx.reshape(-1, 16).T, (8, 1)).astype(np.uint16)


def unstriped(offs):
    return offs[:16].T.reshape(-1).astype(np.int64)


E2M1 = np.array([0.0, 0.5, 1.0, 1.5, 2.0, 3.0, 4.0, 6.0, -0.0, -0.5, -1.0, -1.5, -2.0, -3.0, -4.0, -6.0])


def pack_weight(w, fmt):
    k, n = w.shape
    w = f64(np.asarray(w, np.float32).astype(ml_dtypes.bfloat16)).reshape(k // 32, 32, n)
    amax = np.abs(w).max(1)
    if fmt == "e4m3":
        byte = np.frexp(amax)[1] - 1 + 127 - 7
    else:
        mant, ex = np.frexp(amax / 6.0)
        byte = np.where(mant > 0.5, ex, ex - 1) + 127
    byte = np.clip(np.where(amax > 0, byte, 1), 1, 254)
    scaled = (w * np.exp2(127.0 - byte)[:, None, :]).reshape(k, n).astype(np.float32)
    by_word = np.ascontiguousarray(scaled.reshape(k // 512, 128, 4, n).transpose(0, 1, 3, 2))
    if fmt == "e4m3":
        words = by_word.astype(ml_dtypes.float8_e4m3fn).view(np.uint8)
    else:
        c = by_word.astype(ml_dtypes.float4_e2m1fn).view(np.uint8) & 0xF
        words = (c[..., 0::2] | (c[..., 1::2] << 4)).reshape(k // 512, 128, 2 * n)
    return np.ascontiguousarray(words), np.ascontiguousarray(byte.astype(np.uint8).reshape(k // 512, 16, n))


def unpack_weight(words, scales, fmt):
    g, _, n = scales.shape
    words = np.ascontiguousarray(words).reshape(g, 128, n, -1)
    if fmt == "e4m3":
        vals = words.view(ml_dtypes.float8_e4m3fn).astype(np.float64)
    else:
        nib = np.empty((g, 128, n, 4), np.uint8)
        nib[..., 0::2] = words & 0xF
        nib[..., 1::2] = words >> 4
        vals = E2M1[nib]
    vals = vals * np.repeat(np.exp2(scales.astype(np.float64) - 127.0), 8, axis=1)[..., None]
    return vals.transpose(0, 1, 3, 2).reshape(g * 512, n)


def gelu(v):
    return 0.5 * v * (1.0 + np.tanh(np.sqrt(2.0 / np.pi) * (v + 0.044715 * v**3)))


def striped8(idx):
    return np.concatenate([v.reshape(-1, 16).T for v in idx]).astype(np.uint16)


def unstriped8(offs):
    return np.stack([offs[16 * g:16 * g + 16].T.reshape(-1) for g in range(8)]).astype(np.int64)


def heads(h, wgt, idx8):
    r = np.arange(h.shape[0])
    return wgt[r // 4 % 128] * h[r[:, None], idx8[r % 512 // 64]]


def put_heads(h, wgs, idx8, t2):
    r = np.arange(h.shape[0])
    page = np.zeros((h.shape[0], t2))
    page[r[:, None], idx8[r % 512 // 64]] = wgs[r // 4 % 128] * h
    return page


K, H, N, T, S, P, T2 = 1024, 512, 768, 4096, 1024, 1024, 2048

def setup_inputs():
    n = np.random.standard_normal
    s = mx_kscale(K)[:, None]
    u = mx_kscale(H)[:, None]
    d = {}
    d["tab_words"], d["tab_scales"] = pack_weight(n((K, T)) * s, "e4m3")
    d["offs"] = striped(np.random.permutation(T)[:S])
    d["wa"] = (n((K, H)) / K ** 0.5 / s * u.T).astype(np.float32)
    d["wb_words"], d["wb_scales"] = pack_weight(n((K, H)) / K ** 0.5 / s * u.T, "e2m1")
    d["wc"] = (n((K, H)) / K ** 0.5 / s * u.T).astype(np.float32)
    d["wgs"] = np.repeat(np.random.uniform(0.5, 2.0, (8, S)), 16, axis=0).astype(np.float32)
    d["offs2"] = striped8(np.stack([np.random.permutation(T2)[:S] for _ in range(8)]))
    d["wgt"] = np.repeat(np.random.uniform(0.5, 2.0, (8, P)), 16, axis=0).astype(np.float32)
    d["offs3"] = striped8(np.stack([np.random.permutation(T2)[:P] for _ in range(8)]))
    d["heat"] = (0.8 * n((H, P)) * u).astype(np.float32)
    d["wn_words"], d["wn_scales"] = pack_weight(n((H, N)) / H ** 0.5 / u, "e4m3")
    return d

def reference(tab_words, tab_scales, offs, wa, wb_words, wb_scales, wc, wgs, offs2, wgt, offs3, heat, wn_words, wn_scales):
    v = unpack_weight(tab_words, tab_scales, "e4m3")[:, unstriped(offs)]
    a = mxq(f64(wa), 0, "e4m3").T @ v
    b = unpack_weight(wb_words, wb_scales, "e2m1").T @ v
    cap = mxq(f64(wc), 0, "e4m3").T @ v
    h = np.minimum(np.maximum(a, b), cap)
    page = put_heads(h, f64(wgs), unstriped8(offs2), T2)
    x = heads(page, f64(wgt), unstriped8(offs3))
    z = x - f64(heat)
    y = unpack_weight(wn_words, wn_scales, "e4m3").T @ mxq(z, 0, "e4m3")
    return np.log(1.0 + np.square(y))

@@ -1,0 +1,207 @@
+from contextlib import ExitStack
+
+import concourse.mybir as mybir
+
+K, H, N, T, S, M, T2 = 1024, 512, 768, 4096, 1024, 1024, 2048
+FLOPS = 2 * (3 * K * H * S + H * N * M)
+
+F32 = mybir.dt.float32
+BF16 = mybir.dt.bfloat16
+I32 = mybir.dt.int32
+U32 = mybir.dt.uint32
+U16 = mybir.dt.uint16
+U8 = mybir.dt.uint8
+FP8X4 = mybir.dt.float8_e4m3fn_x4
+FP4X4 = mybir.dt.float4_e2m1fn_x4
+ALU = mybir.AluOpType
+ACT = mybir.ActivationFunctionType
+
+P = 128
+PACK = 4
+PASSES = K // (P * PACK)
+BANK = 512
+HALVES = S // BANK
+QUADS = 4
+SLICES = (128, 256, 256, 128, 128, 128)
+
+
+def tile_list_groove_noise_features_kernel(
+    tc, tab_words, tab_scales, offs, wa, wb_words, wb_scales, wc, wgs, offs2, wgt, offs3, heat, wn_words, wn_scales, out
+):
+    nc = tc.nc
+    with ExitStack() as ctx:
+        keep = ctx.enter_context(tc.tile_pool(name="keep", bufs=1))
+        ring = ctx.enter_context(tc.tile_pool(name="ring", bufs=2))
+        psum = ctx.enter_context(tc.psum_pool(name="psum", bufs=8))
+
+        def held(shape, dtype, name, tag=None):
+            return keep.tile(shape, dtype, name=name, tag=tag or name, align_bytes=64)
+
+        list1 = keep.tile([P, S // 16], U16, name="list1")
+        list2 = keep.tile([P, S // 16], U16, name="list2")
+        list3 = keep.tile([P, M // 16], U16, name="list3")
+
+        rows = PASSES * 16
+        tab_sc = held([P, T], U8, "tab_sc")
+        wb_sc_raw = held([P, H], U8, "wb_sc_raw")
+        staged = held([P, S + H + N], U8, "staged")
+        planes = [held([P, S + H + N], U8, "plane0"), held([P, S + H], U8, "plane1")]
+        tab = [held([P, T], I32, "tab%d" % a) for a in range(PASSES)]
+        wb_raw = held([P, PASSES, 2 * H], U8, "wb_raw")
+        nc.sync.dma_start(list1[:], offs)
+        nc.sync.dma_start(tab_sc[0:rows, :].bitcast(I32), tab_scales.rearrange("a q t -> (a q) t").bitcast(I32))
+        nc.sync.dma_start(wb_sc_raw[0:rows, :].bitcast(I32), wb_scales.rearrange("a q c -> (a q) c").bitcast(I32))
+        nc.sync.dma_start(staged[0:16, S + H :].bitcast(I32), wn_scales[0].bitcast(I32))
+        nc.sync.dma_start(list2[:], offs2)
+        nc.sync.dma_start(list3[:], offs3)
+        nc.sync.dma_start(tab[0][:], tab_words[0].rearrange("p t i -> p (t i)").bitcast(I32))
+        nc.sync.dma_start(wb_raw[:].bitcast(I32), wb_words.rearrange("a p c -> p a c").bitcast(I32))
+        nc.sync.dma_start(tab[1][:], tab_words[1].rearrange("p t i -> p (t i)").bitcast(I32))
+
+        for raw in (tab_sc, wb_sc_raw):
+            nc.vector.memset(raw[32:64, :].bitcast(I32), 0)
+            nc.vector.memset(raw[64:128, :].bitcast(I32), 0)
+        for plane in planes:
+            nc.vector.memset(plane[:].bitcast(I32), 0)
+        pages = [held([P, T2], F32, "page%d" % t) for t in range(2)]
+        for t in range(2):
+            nc.vector.memset(pages[t][:], 0.0)
+
+        nc.vector.tensor_copy(
+            staged[:, S : S + H].rearrange("p (t m) -> p t m", t=PACK), wb_sc_raw[:].rearrange("p (m t) -> p t m", t=PACK)
+        )
+        picked_sc = held([P, S], U8, "picked_sc")
+        nc.vector.tensor_copy(picked_sc[:], tab_sc[:].indirect(list1[:]))
+        nc.vector.tensor_copy(staged[0:rows, 0:S].bitcast(I32), picked_sc[0:rows, :].bitcast(I32))
+        for a in range(PASSES):
+            width = planes[a].shape[1]
+            for q in range(QUADS):
+                row = 16 * a + 4 * q
+                nc.scalar.dma_start(planes[a][32 * q : 32 * q + 4, :].bitcast(I32), staged[row : row + 4, 0:width].bitcast(I32))
+        wn_sc = planes[0][:, S + H :]
+
+        v = {}
+
+        def gather_words(a):
+            for hf in range(HALVES):
+                v[a, hf] = held([P, BANK], U32, "v%d_%d" % (a, hf))
+                cols = slice(hf * BANK // 16, (hf + 1) * BANK // 16)
+                nc.vector.tensor_copy(v[a, hf][:], tab[a][:].bitcast(U32).indirect(list1[:, cols]))
+
+        w_raw = {}
+
+        def load_weight(name, w, a, tag):
+            w_raw[name, a] = held([P, PACK, H], F32, "%s_raw%d" % (name, a), tag)
+            nc.sync.dma_start(
+                w_raw[name, a][:], w[a * P * PACK : (a + 1) * P * PACK, :].rearrange("(p j) c -> p j c", j=PACK)
+            )
+
+        load_weight("wa", wa, 0, "picked_sc")
+        gather_words(0)
+        load_weight("wa", wa, 1, "tab0")
+        wb_sb = held([P, PASSES, PACK, 2 * P], U8, "wb_sb")
+        nc.vector.tensor_copy(
+            wb_sb[:].bitcast(U16), wb_raw[:].bitcast(U16).rearrange("p a (m t) -> p a t m", t=PACK)
+        )
+        load_weight("wc", wc, 0, "wb_raw")
+        gather_words(1)
+        load_weight("wc", wc, 1, "tab1")
+
+        codes, scales = {}, {}
+
+        def quantise_pair(name, a, u, copy):
+            grouped = held([P, 2, P, PACK], BF16, "%s_bf%d_%d" % (name, a, u))
+            copy(
+                grouped[:].rearrange("p t m j -> p m j t"),
+                w_raw[name, a][:].rearrange("p j (m t) -> p m j t", t=PACK)[:, :, :, 2 * u : 2 * u + 2],
+            )
+            codes[name, a, u] = held([P, 2 * P], U32, "%s_q%d_%d" % (name, a, u))
+            scales[name, a, u] = held([P, 2 * P], U8, "%s_s%d_%d" % (name, a, u))
+            nc.vector.quantize_mx(
+                out=codes[name, a, u][:].bitcast(FP8X4),
+                scales=scales[name, a, u][:],
+                in_=grouped[:].rearrange("p t m j -> p (t m j)"),
+            )
+
+        def product(t, hf, stationary):
+            bank = psum.tile([P, BANK], F32, name="bank")
+            for a in range(PASSES):
+                lhs, lhs_sc = stationary(a)
+                nc.tensor.matmul_mx(
+                    out=bank[:], lhsT=lhs, lhsT_scale=lhs_sc,
+                    rhs=v[a, hf][:].bitcast(FP8X4), rhs_scale=planes[a][:, hf * BANK : (hf + 1) * BANK],
+                    start=(a == 0), stop=(a == PASSES - 1),
+                )
+            return bank
+
+        def quantised(name, t):
+            cols = slice((t % 2) * P, (t % 2 + 1) * P)
+            return lambda a: (codes[name, a, t // 2][:, cols].bitcast(FP8X4), scales[name, a, t // 2][:, cols])
+
+        h = [held([P, S], F32, "h%d" % t) for t in range(PACK)]
+        for t in range(PACK):
+            for hf in range(HALVES):
+                bank = product(t, hf, lambda a: (wb_sb[:, a, t, :].bitcast(FP4X4), planes[a][:, S + t * P : S + (t + 1) * P]))
+                nc.scalar.copy(h[t][:, hf * BANK : (hf + 1) * BANK], bank[:])
+
+        for name, op, copy in (("wa", ALU.max, nc.vector.tensor_copy), ("wc", ALU.min, nc.scalar.copy)):
+            for u in range(2):
+                for a in range(PASSES):
+                    quantise_pair(name, a, u, copy)
+            for t in range(PACK):
+                for hf in range(HALVES):
+                    bank = product(t, hf, quantised(name, t))
+                    cols = slice(hf * BANK, (hf + 1) * BANK)
+                    nc.vector.tensor_tensor(h[t][:, cols], bank[:], h[t][:, cols], op)
+
+        wgs_sb = held([P, S], F32, "wgs_sb", "picked_sc")
+        heat_sb = held([P, PACK, M], F32, "heat_sb", "tab0")
+        wgt_sb = held([P, M], F32, "wgt_sb", "wb_raw")
+        wn_sb = held([P, N], I32, "wn_sb", "tab1")
+        nc.sync.dma_start(wgs_sb[:], wgs)
+        nc.sync.dma_start(heat_sb[:], heat.rearrange("(p t) m -> p t m", t=PACK))
+        nc.sync.dma_start(wgt_sb[:], wgt)
+        nc.sync.dma_start(wn_sb[:], wn_words[0].rearrange("p n i -> p (n i)").bitcast(I32))
+
+        for t, tag in ((2, "wc_bf1_1"), (3, "v1_1")):
+            pages.append(held([P, T2], F32, "page%d" % t, tag))
+            nc.gpsimd.memset(pages[t][:], 0.0)
+        for t in range(PACK):
+            nc.vector.tensor_tensor(pages[t][:].indirect(list2[:]), h[t][:], wgs_sb[:], ALU.mult)
+
+        out_v = out.rearrange("(c p) m -> p c m", p=P)
+        m0 = 0
+        for s, w in enumerate(SLICES):
+            cols = slice(m0, m0 + w)
+            x = held([P, PACK, w], F32, "h%d" % (PACK - 1 - s % 2))
+            for t in range(PACK):
+                nc.vector.tensor_tensor(
+                    x[:, t, :], pages[t][:].indirect(list3[:, m0 // 16 : (m0 + w) // 16]), wgt_sb[:, cols], ALU.mult
+                )
+            z = ring.tile([P, w, PACK], BF16, name="z", align_bytes=64)
+            nc.vector.tensor_tensor(
+                z[:].rearrange("p (c i) t -> p c t i", i=2),
+                x[:].rearrange("p t (c i) -> p c t i", i=2),
+                heat_sb[:, :, cols].rearrange("p t (c i) -> p c t i", i=2),
+                ALU.subtract,
+            )
+            zq = ring.tile([P, w], U32, name="zq", align_bytes=64)
+            zs = ring.tile([P, w], U8, name="zs", align_bytes=64)
+            nc.vector.quantize_mx(out=zq[:].bitcast(FP8X4), scales=zs[:], in_=z[:].rearrange("p m t -> p (m t)"))
+            per_bank = BANK // w
+            tiles = N // P
+            for c0 in range(0, tiles, per_bank):
+                n_here = min(per_bank, tiles - c0)
+                bank = psum.tile([P, BANK], F32, name="bank")
+                for k in range(n_here):
+                    ncols = slice((c0 + k) * P, (c0 + k + 1) * P)
+                    nc.tensor.matmul_mx(
+                        out=bank[:, k * w : (k + 1) * w], lhsT=wn_sb[:, ncols].bitcast(FP8X4), lhsT_scale=wn_sc[:, ncols],
+                        rhs=zq[:].bitcast(FP8X4), rhs_scale=zs[:], start=True, stop=True,
+                    )
+                sq = ring.tile([P, n_here * w], F32, name="sq")
+                nc.scalar.activation(sq[:], bank[:, 0 : n_here * w], ACT.Square)
+                res = ring.tile([P, n_here, w], F32, name="res", bufs=4)
+                nc.scalar.activation(res[:].rearrange("p c m -> p (c m)"), sq[:], ACT.Ln, bias=1.0)
+                nc.sync.dma_start(out_v[:, c0 : c0 + n_here, cols], res[:])
+            m0 = m0 + w

@@ -19,10 +19,17 @@ ACT = mybir.ActivationFunctionType
 P = 128
 PACK = 4
 PASSES = K // (P * PACK)
+BLOCKS = 16
+QUADS = 4
+QUAD = P // QUADS
+PER_COLUMN = 16
 BANK = 512
 HALVES = S // BANK
-QUADS = 4
-SLICES = (128, 256, 256, 128, 128, 128)
+PAIRS = PACK // 2
+OUT_TILES = N // P
+STEPS = (128, 256, 256, 128, 128, 128)
+LAST_TILES_PER_BANK = 2
+RESULT_BUFS = 3
 
 
 def tile_list_groove_noise_features_kernel(
@@ -37,11 +44,11 @@ def tile_list_groove_noise_features_kernel(
         def held(shape, dtype, name, tag=None):
             return keep.tile(shape, dtype, name=name, tag=tag or name, align_bytes=64)
 
-        list1 = keep.tile([P, S // 16], U16, name="list1")
-        list2 = keep.tile([P, S // 16], U16, name="list2")
-        list3 = keep.tile([P, M // 16], U16, name="list3")
+        list1 = keep.tile([P, S // PER_COLUMN], U16, name="list1")
+        list2 = keep.tile([P, S // PER_COLUMN], U16, name="list2")
+        list3 = keep.tile([P, M // PER_COLUMN], U16, name="list3")
 
-        rows = PASSES * 16
+        scale_rows = PASSES * BLOCKS
         tab_sc = held([P, T], U8, "tab_sc")
         wb_sc_raw = held([P, H], U8, "wb_sc_raw")
         staged = held([P, S + H + N], U8, "staged")
@@ -49,60 +56,58 @@ def tile_list_groove_noise_features_kernel(
         tab = [held([P, T], I32, "tab%d" % a) for a in range(PASSES)]
         wb_raw = held([P, PASSES, 2 * H], U8, "wb_raw")
         nc.sync.dma_start(list1[:], offs)
-        nc.sync.dma_start(tab_sc[0:rows, :].bitcast(I32), tab_scales.rearrange("a q t -> (a q) t").bitcast(I32))
-        nc.sync.dma_start(wb_sc_raw[0:rows, :].bitcast(I32), wb_scales.rearrange("a q c -> (a q) c").bitcast(I32))
-        nc.sync.dma_start(staged[0:16, S + H :].bitcast(I32), wn_scales[0].bitcast(I32))
-        nc.sync.dma_start(list2[:], offs2)
-        nc.sync.dma_start(list3[:], offs3)
+        nc.scalar.dma_start(tab_sc[0:scale_rows, :].bitcast(I32), tab_scales.rearrange("a q t -> (a q) t").bitcast(I32))
+        nc.scalar.dma_start(wb_sc_raw[0:scale_rows, :].bitcast(I32), wb_scales.rearrange("a q c -> (a q) c").bitcast(I32))
+        nc.scalar.dma_start(staged[0:BLOCKS, S + H :].bitcast(I32), wn_scales[0].bitcast(I32))
         nc.sync.dma_start(tab[0][:], tab_words[0].rearrange("p t i -> p (t i)").bitcast(I32))
         nc.sync.dma_start(wb_raw[:].bitcast(I32), wb_words.rearrange("a p c -> p a c").bitcast(I32))
         nc.sync.dma_start(tab[1][:], tab_words[1].rearrange("p t i -> p (t i)").bitcast(I32))
+        nc.sync.dma_start(list2[:], offs2)
+        nc.sync.dma_start(list3[:], offs3)
 
         for raw in (tab_sc, wb_sc_raw):
-            nc.vector.memset(raw[32:64, :].bitcast(I32), 0)
-            nc.vector.memset(raw[64:128, :].bitcast(I32), 0)
+            nc.vector.memset(raw[scale_rows : P // 2, :].bitcast(I32), 0)
+            nc.vector.memset(raw[P // 2 :, :].bitcast(I32), 0)
         for plane in planes:
             nc.vector.memset(plane[:].bitcast(I32), 0)
         pages = [held([P, T2], F32, "page%d" % t) for t in range(2)]
-        for t in range(2):
-            nc.vector.memset(pages[t][:], 0.0)
+        for page in pages:
+            nc.vector.memset(page[:], 0.0)
 
         nc.vector.tensor_copy(
-            staged[:, S : S + H].rearrange("p (t m) -> p t m", t=PACK), wb_sc_raw[:].rearrange("p (m t) -> p t m", t=PACK)
+            staged[:, S : S + H].rearrange("p (t m) -> p t m", t=PACK),
+            wb_sc_raw[:].rearrange("p (m t) -> p t m", t=PACK),
         )
         picked_sc = held([P, S], U8, "picked_sc")
         nc.vector.tensor_copy(picked_sc[:], tab_sc[:].indirect(list1[:]))
-        nc.vector.tensor_copy(staged[0:rows, 0:S].bitcast(I32), picked_sc[0:rows, :].bitcast(I32))
+        nc.vector.tensor_copy(staged[0:scale_rows, 0:S].bitcast(I32), picked_sc[0:scale_rows, :].bitcast(I32))
         for a in range(PASSES):
             width = planes[a].shape[1]
             for q in range(QUADS):
-                row = 16 * a + 4 * q
-                nc.scalar.dma_start(planes[a][32 * q : 32 * q + 4, :].bitcast(I32), staged[row : row + 4, 0:width].bitcast(I32))
+                row = BLOCKS * a + 4 * q
+                nc.scalar.dma_start(
+                    planes[a][QUAD * q : QUAD * q + 4, :].bitcast(I32), staged[row : row + 4, 0:width].bitcast(I32)
+                )
         wn_sc = planes[0][:, S + H :]
 
-        v = {}
+        picked, w_raw = {}, {}
 
         def gather_words(a):
-            for hf in range(HALVES):
-                v[a, hf] = held([P, BANK], U32, "v%d_%d" % (a, hf))
-                cols = slice(hf * BANK // 16, (hf + 1) * BANK // 16)
-                nc.vector.tensor_copy(v[a, hf][:], tab[a][:].bitcast(U32).indirect(list1[:, cols]))
+            for half in range(HALVES):
+                picked[a, half] = held([P, BANK], U32, "picked%d_%d" % (a, half))
+                entries = slice(half * BANK // PER_COLUMN, (half + 1) * BANK // PER_COLUMN)
+                nc.vector.tensor_copy(picked[a, half][:], tab[a][:].bitcast(U32).indirect(list1[:, entries]))
 
-        w_raw = {}
-
-        def load_weight(name, w, a, tag):
+        def load_weight(name, weight, a, tag):
             w_raw[name, a] = held([P, PACK, H], F32, "%s_raw%d" % (name, a), tag)
-            nc.sync.dma_start(
-                w_raw[name, a][:], w[a * P * PACK : (a + 1) * P * PACK, :].rearrange("(p j) c -> p j c", j=PACK)
-            )
+            rows = weight[a * P * PACK : (a + 1) * P * PACK, :]
+            nc.sync.dma_start(w_raw[name, a][:], rows.rearrange("(p j) c -> p j c", j=PACK))
 
         load_weight("wa", wa, 0, "picked_sc")
         gather_words(0)
         load_weight("wa", wa, 1, "tab0")
         wb_sb = held([P, PASSES, PACK, 2 * P], U8, "wb_sb")
-        nc.vector.tensor_copy(
-            wb_sb[:].bitcast(U16), wb_raw[:].bitcast(U16).rearrange("p a (m t) -> p a t m", t=PACK)
-        )
+        nc.vector.tensor_copy(wb_sb[:].bitcast(U16), wb_raw[:].bitcast(U16).rearrange("p a (m t) -> p a t m", t=PACK))
         load_weight("wc", wc, 0, "wb_raw")
         gather_words(1)
         load_weight("wc", wc, 1, "tab1")
@@ -123,36 +128,40 @@ def tile_list_groove_noise_features_kernel(
                 in_=grouped[:].rearrange("p t m j -> p (t m j)"),
             )
 
-        def product(t, hf, stationary):
+        def stationary(name, t, a):
+            if name == "wb":
+                return wb_sb[:, a, t, :].bitcast(FP4X4), planes[a][:, S + t * P : S + (t + 1) * P]
+            inside = slice((t % 2) * P, (t % 2 + 1) * P)
+            return codes[name, a, t // 2][:, inside].bitcast(FP8X4), scales[name, a, t // 2][:, inside]
+
+        def product(name, t, half):
             bank = psum.tile([P, BANK], F32, name="bank")
             for a in range(PASSES):
-                lhs, lhs_sc = stationary(a)
+                lhs, lhs_sc = stationary(name, t, a)
                 nc.tensor.matmul_mx(
-                    out=bank[:], lhsT=lhs, lhsT_scale=lhs_sc,
-                    rhs=v[a, hf][:].bitcast(FP8X4), rhs_scale=planes[a][:, hf * BANK : (hf + 1) * BANK],
-                    start=(a == 0), stop=(a == PASSES - 1),
+                    out=bank[:],
+                    lhsT=lhs,
+                    lhsT_scale=lhs_sc,
+                    rhs=picked[a, half][:].bitcast(FP8X4),
+                    rhs_scale=planes[a][:, half * BANK : (half + 1) * BANK],
+                    start=(a == 0),
+                    stop=(a == PASSES - 1),
                 )
             return bank
 
-        def quantised(name, t):
-            cols = slice((t % 2) * P, (t % 2 + 1) * P)
-            return lambda a: (codes[name, a, t // 2][:, cols].bitcast(FP8X4), scales[name, a, t // 2][:, cols])
-
         h = [held([P, S], F32, "h%d" % t) for t in range(PACK)]
         for t in range(PACK):
-            for hf in range(HALVES):
-                bank = product(t, hf, lambda a: (wb_sb[:, a, t, :].bitcast(FP4X4), planes[a][:, S + t * P : S + (t + 1) * P]))
-                nc.scalar.copy(h[t][:, hf * BANK : (hf + 1) * BANK], bank[:])
+            for half in range(HALVES):
+                nc.scalar.copy(h[t][:, half * BANK : (half + 1) * BANK], product("wb", t, half)[:])
 
         for name, op, copy in (("wa", ALU.max, nc.vector.tensor_copy), ("wc", ALU.min, nc.scalar.copy)):
-            for u in range(2):
+            for u in range(PAIRS):
                 for a in range(PASSES):
                     quantise_pair(name, a, u, copy)
             for t in range(PACK):
-                for hf in range(HALVES):
-                    bank = product(t, hf, quantised(name, t))
-                    cols = slice(hf * BANK, (hf + 1) * BANK)
-                    nc.vector.tensor_tensor(h[t][:, cols], bank[:], h[t][:, cols], op)
+                for half in range(HALVES):
+                    part = h[t][:, half * BANK : (half + 1) * BANK]
+                    nc.vector.tensor_tensor(part, product(name, t, half)[:], part, op)
 
         wgs_sb = held([P, S], F32, "wgs_sb", "picked_sc")
         heat_sb = held([P, PACK, M], F32, "heat_sb", "tab0")
@@ -163,21 +172,21 @@ def tile_list_groove_noise_features_kernel(
         nc.sync.dma_start(wgt_sb[:], wgt)
         nc.sync.dma_start(wn_sb[:], wn_words[0].rearrange("p n i -> p (n i)").bitcast(I32))
 
-        for t, tag in ((2, "wc_bf1_1"), (3, "v1_1")):
+        for t, tag in ((2, "wc_bf1_1"), (3, "picked1_1")):
             pages.append(held([P, T2], F32, "page%d" % t, tag))
             nc.gpsimd.memset(pages[t][:], 0.0)
+
         for t in range(PACK):
             nc.vector.tensor_tensor(pages[t][:].indirect(list2[:]), h[t][:], wgs_sb[:], ALU.mult)
 
         out_v = out.rearrange("(c p) m -> p c m", p=P)
         m0 = 0
-        for s, w in enumerate(SLICES):
+        for s, w in enumerate(STEPS):
             cols = slice(m0, m0 + w)
-            x = held([P, PACK, w], F32, "h%d" % (PACK - 1 - s % 2))
+            entries = slice(m0 // PER_COLUMN, (m0 + w) // PER_COLUMN)
+            x = held([P, PACK, w], F32, "x", "h%d" % (PACK - 1 - s % 2))
             for t in range(PACK):
-                nc.vector.tensor_tensor(
-                    x[:, t, :], pages[t][:].indirect(list3[:, m0 // 16 : (m0 + w) // 16]), wgt_sb[:, cols], ALU.mult
-                )
+                nc.vector.tensor_tensor(x[:, t, :], pages[t][:].indirect(list3[:, entries]), wgt_sb[:, cols], ALU.mult)
             z = ring.tile([P, w, PACK], BF16, name="z", align_bytes=64)
             nc.vector.tensor_tensor(
                 z[:].rearrange("p (c i) t -> p c t i", i=2),
@@ -185,23 +194,39 @@ def tile_list_groove_noise_features_kernel(
                 heat_sb[:, :, cols].rearrange("p t (c i) -> p c t i", i=2),
                 ALU.subtract,
             )
-            zq = ring.tile([P, w], U32, name="zq", align_bytes=64)
-            zs = ring.tile([P, w], U8, name="zs", align_bytes=64)
-            nc.vector.quantize_mx(out=zq[:].bitcast(FP8X4), scales=zs[:], in_=z[:].rearrange("p m t -> p (m t)"))
-            per_bank = BANK // w
-            tiles = N // P
-            for c0 in range(0, tiles, per_bank):
-                n_here = min(per_bank, tiles - c0)
+            z_codes = ring.tile([P, w], U32, name="z_codes", align_bytes=64)
+            z_scales = ring.tile([P, w], U8, name="z_scales", align_bytes=64)
+            nc.vector.quantize_mx(
+                out=z_codes[:].bitcast(FP8X4), scales=z_scales[:], in_=z[:].rearrange("p m t -> p (m t)")
+            )
+
+            last = s == len(STEPS) - 1
+            per_bank = LAST_TILES_PER_BANK if last else BANK // w
+            squares = ring.tile([P, OUT_TILES * w], F32, name="squares")
+            res = ring.tile([P, OUT_TILES, w], F32, name="res", bufs=RESULT_BUFS)
+
+            def finish(c0, c1):
+                nc.scalar.activation(
+                    res[:, c0:c1, :].rearrange("p c m -> p (c m)"), squares[:, c0 * w : c1 * w], ACT.Ln, bias=1.0
+                )
+                nc.sync.dma_start(out_v[:, c0:c1, cols], res[:, c0:c1, :])
+
+            for c0 in range(0, OUT_TILES, per_bank):
+                c1 = min(c0 + per_bank, OUT_TILES)
                 bank = psum.tile([P, BANK], F32, name="bank")
-                for k in range(n_here):
-                    ncols = slice((c0 + k) * P, (c0 + k + 1) * P)
+                for c in range(c0, c1):
                     nc.tensor.matmul_mx(
-                        out=bank[:, k * w : (k + 1) * w], lhsT=wn_sb[:, ncols].bitcast(FP8X4), lhsT_scale=wn_sc[:, ncols],
-                        rhs=zq[:].bitcast(FP8X4), rhs_scale=zs[:], start=True, stop=True,
+                        out=bank[:, (c - c0) * w : (c - c0 + 1) * w],
+                        lhsT=wn_sb[:, c * P : (c + 1) * P].bitcast(FP8X4),
+                        lhsT_scale=wn_sc[:, c * P : (c + 1) * P],
+                        rhs=z_codes[:].bitcast(FP8X4),
+                        rhs_scale=z_scales[:],
+                        start=True,
+                        stop=True,
                     )
-                sq = ring.tile([P, n_here * w], F32, name="sq")
-                nc.scalar.activation(sq[:], bank[:, 0 : n_here * w], ACT.Square)
-                res = ring.tile([P, n_here, w], F32, name="res", bufs=4)
-                nc.scalar.activation(res[:].rearrange("p c m -> p (c m)"), sq[:], ACT.Ln, bias=1.0)
-                nc.sync.dma_start(out_v[:, c0 : c0 + n_here, cols], res[:])
+                nc.scalar.activation(squares[:, c0 * w : c1 * w], bank[:, 0 : (c1 - c0) * w], ACT.Square)
+                if last:
+                    finish(c0, c1)
+            if not last:
+                finish(0, OUT_TILES)
             m0 = m0 + w

from contextlib import ExitStack

import concourse.mybir as mybir

K, H, N, T, S, M, T2 = 1024, 512, 768, 4096, 1024, 1024, 2048
FLOPS = 2 * (3 * K * H * S + H * N * M)

F32 = mybir.dt.float32
BF16 = mybir.dt.bfloat16
I32 = mybir.dt.int32
U32 = mybir.dt.uint32
U16 = mybir.dt.uint16
U8 = mybir.dt.uint8
FP8X4 = mybir.dt.float8_e4m3fn_x4
FP4X4 = mybir.dt.float4_e2m1fn_x4
ALU = mybir.AluOpType
ACT = mybir.ActivationFunctionType

P = 128
PACK = 4
PASSES = K // (P * PACK)
BLOCKS = 16
QUADS = 4
QUAD = P // QUADS
PER_COLUMN = 16
BANK = 512
HALVES = S // BANK
PAIRS = PACK // 2
OUT_TILES = N // P
STEPS = (128, 256, 256, 128, 128, 128)
LAST_TILES_PER_BANK = 2
RESULT_BUFS = 3


def tile_list_groove_noise_features_kernel(
    tc, tab_words, tab_scales, offs, wa, wb_words, wb_scales, wc, wgs, offs2, wgt, offs3, heat, wn_words, wn_scales, out
):
    nc = tc.nc
    with ExitStack() as ctx:
        keep = ctx.enter_context(tc.tile_pool(name="keep", bufs=1))
        ring = ctx.enter_context(tc.tile_pool(name="ring", bufs=2))
        psum = ctx.enter_context(tc.psum_pool(name="psum", bufs=8))

        def held(shape, dtype, name, tag=None):
            return keep.tile(shape, dtype, name=name, tag=tag or name, align_bytes=64)

        list1 = keep.tile([P, S // PER_COLUMN], U16, name="list1")
        list2 = keep.tile([P, S // PER_COLUMN], U16, name="list2")
        list3 = keep.tile([P, M // PER_COLUMN], U16, name="list3")

        scale_rows = PASSES * BLOCKS
        tab_sc = held([P, T], U8, "tab_sc")
        wb_sc_raw = held([P, H], U8, "wb_sc_raw")
        staged = held([P, S + H + N], U8, "staged")
        planes = [held([P, S + H + N], U8, "plane0"), held([P, S + H], U8, "plane1")]
        tab = [held([P, T], I32, "tab%d" % a) for a in range(PASSES)]
        wb_raw = held([P, PASSES, 2 * H], U8, "wb_raw")
        nc.sync.dma_start(list1[:], offs)
        nc.scalar.dma_start(tab_sc[0:scale_rows, :].bitcast(I32), tab_scales.rearrange("a q t -> (a q) t").bitcast(I32))
        nc.scalar.dma_start(wb_sc_raw[0:scale_rows, :].bitcast(I32), wb_scales.rearrange("a q c -> (a q) c").bitcast(I32))
        nc.scalar.dma_start(staged[0:BLOCKS, S + H :].bitcast(I32), wn_scales[0].bitcast(I32))
        nc.sync.dma_start(tab[0][:], tab_words[0].rearrange("p t i -> p (t i)").bitcast(I32))
        nc.sync.dma_start(wb_raw[:].bitcast(I32), wb_words.rearrange("a p c -> p a c").bitcast(I32))
        nc.sync.dma_start(tab[1][:], tab_words[1].rearrange("p t i -> p (t i)").bitcast(I32))
        nc.sync.dma_start(list2[:], offs2)
        nc.sync.dma_start(list3[:], offs3)

        for raw in (tab_sc, wb_sc_raw):
            nc.vector.memset(raw[scale_rows : P // 2, :].bitcast(I32), 0)
            nc.vector.memset(raw[P // 2 :, :].bitcast(I32), 0)
        for plane in planes:
            nc.vector.memset(plane[:].bitcast(I32), 0)
        pages = [held([P, T2], F32, "page%d" % t) for t in range(2)]
        for page in pages:
            nc.vector.memset(page[:], 0.0)

        nc.vector.tensor_copy(
            staged[:, S : S + H].rearrange("p (t m) -> p t m", t=PACK),
            wb_sc_raw[:].rearrange("p (m t) -> p t m", t=PACK),
        )
        picked_sc = held([P, S], U8, "picked_sc")
        nc.vector.tensor_copy(picked_sc[:], tab_sc[:].indirect(list1[:]))
        nc.vector.tensor_copy(staged[0:scale_rows, 0:S].bitcast(I32), picked_sc[0:scale_rows, :].bitcast(I32))
        for a in range(PASSES):
            width = planes[a].shape[1]
            for q in range(QUADS):
                row = BLOCKS * a + 4 * q
                nc.scalar.dma_start(
                    planes[a][QUAD * q : QUAD * q + 4, :].bitcast(I32), staged[row : row + 4, 0:width].bitcast(I32)
                )
        wn_sc = planes[0][:, S + H :]

        picked, w_raw = {}, {}

        def gather_words(a):
            for half in range(HALVES):
                picked[a, half] = held([P, BANK], U32, "picked%d_%d" % (a, half))
                entries = slice(half * BANK // PER_COLUMN, (half + 1) * BANK // PER_COLUMN)
                nc.vector.tensor_copy(picked[a, half][:], tab[a][:].bitcast(U32).indirect(list1[:, entries]))

        def load_weight(name, weight, a, tag):
            w_raw[name, a] = held([P, PACK, H], F32, "%s_raw%d" % (name, a), tag)
            rows = weight[a * P * PACK : (a + 1) * P * PACK, :]
            nc.sync.dma_start(w_raw[name, a][:], rows.rearrange("(p j) c -> p j c", j=PACK))

        load_weight("wa", wa, 0, "picked_sc")
        gather_words(0)
        load_weight("wa", wa, 1, "tab0")
        wb_sb = held([P, PASSES, PACK, 2 * P], U8, "wb_sb")
        nc.vector.tensor_copy(wb_sb[:].bitcast(U16), wb_raw[:].bitcast(U16).rearrange("p a (m t) -> p a t m", t=PACK))
        load_weight("wc", wc, 0, "wb_raw")
        gather_words(1)
        load_weight("wc", wc, 1, "tab1")

        codes, scales = {}, {}

        def quantise_pair(name, a, u, copy):
            grouped = held([P, 2, P, PACK], BF16, "%s_bf%d_%d" % (name, a, u))
            copy(
                grouped[:].rearrange("p t m j -> p m j t"),
                w_raw[name, a][:].rearrange("p j (m t) -> p m j t", t=PACK)[:, :, :, 2 * u : 2 * u + 2],
            )
            codes[name, a, u] = held([P, 2 * P], U32, "%s_q%d_%d" % (name, a, u))
            scales[name, a, u] = held([P, 2 * P], U8, "%s_s%d_%d" % (name, a, u))
            nc.vector.quantize_mx(
                out=codes[name, a, u][:].bitcast(FP8X4),
                scales=scales[name, a, u][:],
                in_=grouped[:].rearrange("p t m j -> p (t m j)"),
            )

        def stationary(name, t, a):
            if name == "wb":
                return wb_sb[:, a, t, :].bitcast(FP4X4), planes[a][:, S + t * P : S + (t + 1) * P]
            inside = slice((t % 2) * P, (t % 2 + 1) * P)
            return codes[name, a, t // 2][:, inside].bitcast(FP8X4), scales[name, a, t // 2][:, inside]

        def product(name, t, half):
            bank = psum.tile([P, BANK], F32, name="bank")
            for a in range(PASSES):
                lhs, lhs_sc = stationary(name, t, a)
                nc.tensor.matmul_mx(
                    out=bank[:],
                    lhsT=lhs,
                    lhsT_scale=lhs_sc,
                    rhs=picked[a, half][:].bitcast(FP8X4),
                    rhs_scale=planes[a][:, half * BANK : (half + 1) * BANK],
                    start=(a == 0),
                    stop=(a == PASSES - 1),
                )
            return bank

        h = [held([P, S], F32, "h%d" % t) for t in range(PACK)]
        for t in range(PACK):
            for half in range(HALVES):
                nc.scalar.copy(h[t][:, half * BANK : (half + 1) * BANK], product("wb", t, half)[:])

        for name, op, copy in (("wa", ALU.max, nc.vector.tensor_copy), ("wc", ALU.min, nc.scalar.copy)):
            for u in range(PAIRS):
                for a in range(PASSES):
                    quantise_pair(name, a, u, copy)
            for t in range(PACK):
                for half in range(HALVES):
                    part = h[t][:, half * BANK : (half + 1) * BANK]
                    nc.vector.tensor_tensor(part, product(name, t, half)[:], part, op)

        wgs_sb = held([P, S], F32, "wgs_sb", "picked_sc")
        heat_sb = held([P, PACK, M], F32, "heat_sb", "tab0")
        wgt_sb = held([P, M], F32, "wgt_sb", "wb_raw")
        wn_sb = held([P, N], I32, "wn_sb", "tab1")
        nc.sync.dma_start(wgs_sb[:], wgs)
        nc.sync.dma_start(heat_sb[:], heat.rearrange("(p t) m -> p t m", t=PACK))
        nc.sync.dma_start(wgt_sb[:], wgt)
        nc.sync.dma_start(wn_sb[:], wn_words[0].rearrange("p n i -> p (n i)").bitcast(I32))

        for t, tag in ((2, "wc_bf1_1"), (3, "picked1_1")):
            pages.append(held([P, T2], F32, "page%d" % t, tag))
            nc.gpsimd.memset(pages[t][:], 0.0)

        for t in range(PACK):
            nc.vector.tensor_tensor(pages[t][:].indirect(list2[:]), h[t][:], wgs_sb[:], ALU.mult)

        out_v = out.rearrange("(c p) m -> p c m", p=P)
        m0 = 0
        for s, w in enumerate(STEPS):
            cols = slice(m0, m0 + w)
            entries = slice(m0 // PER_COLUMN, (m0 + w) // PER_COLUMN)
            x = held([P, PACK, w], F32, "x", "h%d" % (PACK - 1 - s % 2))
            for t in range(PACK):
                nc.vector.tensor_tensor(x[:, t, :], pages[t][:].indirect(list3[:, entries]), wgt_sb[:, cols], ALU.mult)
            z = ring.tile([P, w, PACK], BF16, name="z", align_bytes=64)
            nc.vector.tensor_tensor(
                z[:].rearrange("p (c i) t -> p c t i", i=2),
                x[:].rearrange("p t (c i) -> p c t i", i=2),
                heat_sb[:, :, cols].rearrange("p t (c i) -> p c t i", i=2),
                ALU.subtract,
            )
            z_codes = ring.tile([P, w], U32, name="z_codes", align_bytes=64)
            z_scales = ring.tile([P, w], U8, name="z_scales", align_bytes=64)
            nc.vector.quantize_mx(
                out=z_codes[:].bitcast(FP8X4), scales=z_scales[:], in_=z[:].rearrange("p m t -> p (m t)")
            )

            last = s == len(STEPS) - 1
            per_bank = LAST_TILES_PER_BANK if last else BANK // w
            squares = ring.tile([P, OUT_TILES * w], F32, name="squares")
            res = ring.tile([P, OUT_TILES, w], F32, name="res", bufs=RESULT_BUFS)

            def finish(c0, c1):
                nc.scalar.activation(
                    res[:, c0:c1, :].rearrange("p c m -> p (c m)"), squares[:, c0 * w : c1 * w], ACT.Ln, bias=1.0
                )
                nc.sync.dma_start(out_v[:, c0:c1, cols], res[:, c0:c1, :])

            for c0 in range(0, OUT_TILES, per_bank):
                c1 = min(c0 + per_bank, OUT_TILES)
                bank = psum.tile([P, BANK], F32, name="bank")
                for c in range(c0, c1):
                    nc.tensor.matmul_mx(
                        out=bank[:, (c - c0) * w : (c - c0 + 1) * w],
                        lhsT=wn_sb[:, c * P : (c + 1) * P].bitcast(FP8X4),
                        lhsT_scale=wn_sc[:, c * P : (c + 1) * P],
                        rhs=z_codes[:].bitcast(FP8X4),
                        rhs_scale=z_scales[:],
                        start=True,
                        stop=True,
                    )
                nc.scalar.activation(squares[:, c0 * w : c1 * w], bank[:, 0 : (c1 - c0) * w], ACT.Square)
                if last:
                    finish(c0, c1)
            if not last:
                finish(0, OUT_TILES)
            m0 = m0 + w
